import numpy as np
import ml_dtypes


def mxq(x, axis, fmt="e4m3"):
    dtype, down = {"e4m3": (ml_dtypes.float8_e4m3fn, 7), "e5m2": (ml_dtypes.float8_e5m2, 14)}[fmt]
    v = np.moveaxis(np.asarray(x, np.float32).astype(ml_dtypes.bfloat16).astype(np.float64), axis, -1)
    blocks = v.reshape(v.shape[:-1] + (-1, 32))
    amax = np.abs(blocks).max(-1, keepdims=True)
    byte = np.maximum(np.where(amax > 0, np.frexp(amax)[1] - 1 + 127, 0) - down, 1)
    scale = np.exp2(byte - 127.0)
    codes = (blocks / scale).astype(np.float32).astype(dtype).astype(np.float64)
    return np.moveaxis((codes * scale).reshape(v.shape), -1, axis)


WIDE = False


def mx_kscale(k):
    if not WIDE:
        return np.ones(k)
    levels = np.array([10, -10, 5, -5, 0])
    if k % 512:
        return np.exp2(np.random.permutation(np.resize(levels, k // 32))).repeat(32)
    a = np.empty((k // 512, 16))
    for p in range(k // 512):
        a[p, :8] = np.random.permutation(np.resize(levels, 8))
        for g in range(8):
            far = levels[np.abs(levels - a[p, g]) >= 10]
            a[p, g + 8] = far[np.random.randint(len(far))]
    return np.exp2(a.ravel()).repeat(32)


def f64(x):
    return np.asarray(x).astype(np.float64)


def striped(idx):
    return np.tile(idx.reshape(-1, 16).T, (8, 1)).astype(np.uint16)


def unstriped(offs):
    return offs[:16].T.reshape(-1).astype(np.int64)


def pack_weight(w):
    k, n = w.shape
    w = f64(np.asarray(w, np.float32).astype(ml_dtypes.bfloat16)).reshape(k // 32, 32, n)
    amax = np.abs(w).max(1)
    byte = np.clip(np.where(amax > 0, np.frexp(amax)[1] - 1 + 127 - 7, 1), 1, 254)
    scaled = (w * np.exp2(127.0 - byte)[:, None, :]).reshape(k, n).astype(np.float32)
    words = np.ascontiguousarray(scaled.reshape(k // 512, 128, 4, n).transpose(0, 1, 3, 2)).astype(ml_dtypes.float8_e4m3fn).view(np.uint8)
    return words, np.ascontiguousarray(byte.astype(np.uint8).reshape(k // 512, 16, n))


def unpack_weight(words, scales):
    g, p, n, _ = words.shape
    vals = np.ascontiguousarray(words).view(ml_dtypes.float8_e4m3fn).astype(np.float64) * np.repeat(np.exp2(scales.astype(np.float64) - 127.0), 8, axis=1)[..., None]
    return vals.transpose(0, 1, 3, 2).reshape(g * 512, n)


E2M1 = np.array([0.0, 0.5, 1.0, 1.5, 2.0, 3.0, 4.0, 6.0, -0.0, -0.5, -1.0, -1.5, -2.0, -3.0, -4.0, -6.0])


def pack_fp4(w):
    k, n = w.shape
    w = f64(np.asarray(w, np.float32).astype(ml_dtypes.bfloat16)).reshape(k // 32, 32, n)
    amax = np.abs(w).max(1)
    mant, ex = np.frexp(amax / 6.0)
    byte = np.clip(np.where(amax > 0, np.where(mant > 0.5, ex, ex - 1) + 127, 1), 1, 254)
    scaled = (w * np.exp2(127.0 - byte)[:, None, :]).reshape(k, n).astype(np.float32)
    c = np.ascontiguousarray(scaled.reshape(k // 512, 128, 4, n).transpose(0, 1, 3, 2)).astype(ml_dtypes.float4_e2m1fn).view(np.uint8) & 0xF
    words = (c[..., 0::2] | (c[..., 1::2] << 4)).reshape(k // 512, 128, 2 * n)
    return np.ascontiguousarray(words), np.ascontiguousarray(byte.astype(np.uint8).reshape(k // 512, 16, n))


def unpack_fp4(words, scales):
    g, _, n = scales.shape
    words = np.ascontiguousarray(words).reshape(g, 128, n, 2)
    nib = np.empty((g, 128, n, 4), np.uint8)
    nib[..., 0::2] = words & 0xF
    nib[..., 1::2] = words >> 4
    vals = E2M1[nib] * np.repeat(np.exp2(scales.astype(np.float64) - 127.0), 8, axis=1)[..., None]
    return vals.transpose(0, 1, 3, 2).reshape(g * 512, n)


def sigmoid(v):
    return 1.0 / (1.0 + np.exp(-np.maximum(v, -700.0)))


K, T, S, N, H, U = 512, 1024, 512, 256, 512, 1024


def setup_inputs():
    n = np.random.standard_normal
    s = mx_kscale(K)[:, None]
    u = mx_kscale(H)
    packed_xT = pack_weight(n((K, T)) * s)
    packed_w1 = pack_fp4(n((K, H)) / np.sqrt(K) / s)
    packed_w2 = pack_fp4(n((K, H)) / np.sqrt(K) / s)
    packed_w3 = pack_fp4(n((H, N)) / np.sqrt(H) / u[:, None])
    return {
        "x_words": packed_xT[0],
        "x_scales": packed_xT[1],
        "w1_words": packed_w1[0],
        "w1_scales": packed_w1[1],
        "w2_words": packed_w2[0],
        "w2_scales": packed_w2[1],
        "page": (n((H, U))).astype(np.float32),
        "ref": (n((H, U))).astype(np.float32),
        "unit": (np.random.uniform(0.6, 1.4, (H, 1)) * u[:, None]).astype(np.float32),
        "w3_words": packed_w3[0],
        "w3_scales": packed_w3[1],
        "offs": striped(np.random.permutation(T)[:S]),
        "at": striped(np.random.permutation(U)[:S]),
        "cop": striped(np.random.permutation(S)),
        "rd": striped(np.random.permutation(U)),
    }


def reference(x_words, x_scales, w1_words, w1_scales, w2_words, w2_scales, page, ref, unit, w3_words, w3_scales, offs, at, cop, rd):
    xq = unpack_weight(x_words, x_scales)[:, unstriped(offs)]
    yg = unpack_fp4(w2_words, w2_scales).T @ xq
    fg = sigmoid(yg)
    old = f64(page)[:, unstriped(at)]
    y = unpack_fp4(w1_words, w1_scales).T @ xq
    neww = fg * old + (-1.0 * fg + 1.0) * np.tanh(y)
    ncp = neww[:, unstriped(cop)]
    wr = neww + 0.5 * ncp
    pnew = f64(page).copy()
    pnew[:, unstriped(at)] = wr
    read = pnew[:, unstriped(rd)]
    dz = read - f64(ref)
    hid = f64(unit) * (read * sigmoid(dz))
    return unpack_fp4(w3_words, w3_scales).T @ mxq(hid, 0, "e4m3")

@@ -1,0 +1,239 @@
+from contextlib import ExitStack
+
+import concourse.mybir as mybir
+from concourse.masks import make_identity
+
+K, T, S, N, H, U = 512, 1024, 512, 256, 512, 1024
+FLOPS = 2 * K * H * S * 2 + 2 * H * N * U
+
+F32 = mybir.dt.float32
+BF16 = mybir.dt.bfloat16
+I32 = mybir.dt.int32
+U32 = mybir.dt.uint32
+U16 = mybir.dt.uint16
+U8 = mybir.dt.uint8
+FP8X4 = mybir.dt.float8_e4m3fn_x4
+FP4X4 = mybir.dt.float4_e2m1fn_x4
+ACT = mybir.ActivationFunctionType
+ALU = mybir.AluOpType
+
+P = 128
+PACK = 4
+BANK = 512
+OUT_COLS = 256
+
+
+def load_scale_rows(queue, plane, scales):
+    for q in range(4):
+        queue.dma_start(out=plane[32 * q : 32 * q + 4, :].bitcast(I32), in_=scales[0, 4 * q : 4 * q + 4, :].bitcast(I32))
+
+
+def tile_picked_yrwpage_gate_p_kernel(
+    tc, x_words, x_scales, w1_words, w1_scales, w2_words, w2_scales, page, ref, unit, w3_words, w3_scales, offs, at, cop, rd, out
+):
+    nc = tc.nc
+    with ExitStack() as ctx:
+        keep = ctx.enter_context(tc.tile_pool(name="keep", bufs=1))
+        work = ctx.enter_context(tc.tile_pool(name="work", bufs=2))
+        psum = ctx.enter_context(tc.psum_pool(name="psum", bufs=2))
+
+        offs_sb = keep.tile([P, S // 16], U16, name="offs_sb")
+        at_sb = keep.tile([P, S // 16], U16, name="at_sb")
+        cop_sb = keep.tile([P, S // 16], U16, name="cop_sb")
+        rd_sb = keep.tile([P, U // 16], U16, name="rd_sb")
+        xw = keep.tile([P, T], U32, name="xw", align_bytes=64)
+        xs = keep.tile([P, T], U8, name="xs", align_bytes=64)
+        w1w = keep.tile([P, 2 * H], U8, name="w1w", align_bytes=64)
+        w2w = keep.tile([P, 2 * H], U8, name="w2w", align_bytes=64)
+        w3w = keep.tile([P, 2 * N], U8, name="w3w", align_bytes=64)
+        w1s = keep.tile([P, H], U8, name="w1s", align_bytes=64)
+        w2s = keep.tile([P, H], U8, name="w2s", align_bytes=64)
+        w3s = keep.tile([P, N], U8, name="w3s", align_bytes=64)
+        unit_sb = keep.tile([P, PACK], F32, name="unit_sb")
+        pages = [keep.tile([P, U], F32, name="page%d" % t) for t in range(PACK)]
+        refs = [keep.tile([P, U], F32, name="ref%d" % t) for t in range(PACK)]
+        page_rows = page.rearrange("(p t) c -> t p c", t=PACK)
+        ref_rows = ref.rearrange("(p t) c -> t p c", t=PACK)
+
+        for plane in (xs, w1s, w2s, w3s):
+            nc.vector.memset(plane[:].bitcast(I32), 0)
+
+        nc.sync.dma_start(offs_sb[:], offs)
+        nc.sync.dma_start(out=xw[:].bitcast(I32), in_=x_words[0].rearrange("p n t -> p (n t)").bitcast(I32))
+        load_scale_rows(nc.sync, xs, x_scales)
+        load_scale_rows(nc.gpsimd, w1s, w1_scales)
+        nc.sync.dma_start(out=w1w[:].bitcast(I32), in_=w1_words[0].bitcast(I32))
+        nc.sync.dma_start(out=w2w[:].bitcast(I32), in_=w2_words[0].bitcast(I32))
+        nc.sync.dma_start(at_sb[:], at)
+        nc.sync.dma_start(out=pages[0][:], in_=page_rows[0])
+        load_scale_rows(nc.sync, w2s, w2_scales)
+        nc.sync.dma_start(cop_sb[:], cop)
+        for t in range(1, PACK):
+            nc.sync.dma_start(out=pages[t][:], in_=page_rows[t])
+        nc.sync.dma_start(rd_sb[:], rd)
+        nc.sync.dma_start(out=unit_sb[:], in_=unit.rearrange("(p t) o -> p (t o)", t=PACK))
+        for t in range(PACK):
+            nc.sync.dma_start(out=refs[t][:], in_=ref_rows[t])
+        nc.sync.dma_start(out=w3w[:].bitcast(I32), in_=w3_words[0].bitcast(I32))
+        load_scale_rows(nc.sync, w3s, w3_scales)
+
+        ident = keep.tile([P, P], F32, name="ident")
+        make_identity(nc, ident[:])
+        neg_unit = keep.tile([P, PACK], F32, name="neg_unit")
+        nc.gpsimd.tensor_scalar(neg_unit[:], unit_sb[:], -1.0, 0.0, ALU.mult, ALU.add)
+
+        xq = keep.tile([P, S], U32, name="xq", align_bytes=64)
+        xqs = keep.tile([P, S], U8, name="xqs", align_bytes=64)
+        nc.vector.tensor_copy(xqs[:], xs[:].indirect(offs_sb[:]))
+        nc.vector.tensor_copy(xq[:], xw[:].indirect(offs_sb[:]))
+
+        dealt = []
+        for name, words, scales in (("w1", w1w, w1s), ("w2", w2w, w2s)):
+            words_d = keep.tile([P, 2 * H], U8, name=name + "wd", align_bytes=64)
+            scales_d = keep.tile([P, H], U8, name=name + "sd", align_bytes=64)
+            nc.scalar.copy(
+                words_d[:].bitcast(U16).rearrange("p (t m) -> p t m", t=PACK),
+                words[:].bitcast(U16).rearrange("p (m t) -> p t m", t=PACK),
+            )
+            nc.vector.tensor_copy(
+                scales_d[:].rearrange("p (t m) -> p t m", t=PACK),
+                scales[:].rearrange("p (m t) -> p t m", t=PACK),
+            )
+            dealt.append((words_d, scales_d))
+
+        def product(t, which):
+            words_d, scales_d = dealt[which]
+            acc = psum.tile([P, S], F32, name="acc", bufs=5)
+            nc.tensor.matmul_mx(
+                out=acc[:],
+                lhsT=words_d[:, 2 * P * t : 2 * P * (t + 1)].bitcast(FP4X4),
+                lhsT_scale=scales_d[:, P * t : P * (t + 1)],
+                rhs=xq[:].bitcast(FP8X4),
+                rhs_scale=xqs[:],
+                start=True,
+                stop=True,
+            )
+            return acc
+
+        def activations(t):
+            y = product(t, 0)
+            yg = product(t, 1)
+            fg = work.tile([P, S], F32, name="fg", bufs=4)
+            th = work.tile([P, S], F32, name="th", bufs=4)
+            old = None
+            if t == 0:
+                old = keep.tile([P, S], F32, name="old")
+                nc.scalar.activation(old[:], pages[t][:].indirect(at_sb[:]), ACT.Copy)
+            nc.scalar.activation(th[:], y[:], ACT.Tanh)
+            nc.scalar.activation(fg[:], yg[:], ACT.Sigmoid)
+            return fg, th, old
+
+        halves = [slice(0, S // 2), slice(S // 2, S)]
+        list_halves = [slice(0, S // 32), slice(S // 32, S // 16)]
+
+        def blend(t, fg, th, old):
+            diff = work.tile([P, S], F32, name="diff")
+            kept = work.tile([P, S], F32, name="kept")
+            neww = work.tile([P, S], F32, name="neww", bufs=4)
+            for cols, entries in zip(halves, list_halves):
+                source = old[:, cols] if t == 0 else pages[t][:].indirect(at_sb[:, entries])
+                nc.vector.tensor_tensor(diff[:, cols], source, th[:, cols], ALU.subtract)
+            for cols in halves:
+                nc.vector.tensor_tensor(kept[:, cols], diff[:, cols], fg[:, cols], ALU.mult)
+            for cols in halves:
+                nc.vector.tensor_tensor(neww[:, cols], kept[:, cols], th[:, cols], ALU.add)
+            return neww
+
+        def copied(neww):
+            half = work.tile([P, S], F32, name="half", bufs=4)
+            for cols, entries in zip(halves, list_halves):
+                nc.scalar.activation(half[:, cols], neww[:].indirect(cop_sb[:, entries]), ACT.Copy, scale=0.5)
+            return half
+
+        def write_back(t, neww, half):
+            nc.vector.tensor_tensor(pages[t][:].indirect(at_sb[:]), neww[:], half[:], ALU.add)
+
+        hid_rows = [keep.tile([P, PACK, BANK], BF16, name="hid_rows%d" % h, align_bytes=64) for h in range(U // BANK)]
+
+        def read_rows(t, h):
+            neg_read = work.tile([P, BANK], F32, name="neg_read", bufs=8)
+            nc.scalar.activation(neg_read[:], pages[t][:].indirect(rd_sb[:, h * 32 : (h + 1) * 32]), ACT.Copy, scale=-1.0)
+            neg_dz = psum.tile([P, BANK], F32, name="neg_dz", bufs=3)
+            blocks = BANK // P
+            for c in range(blocks):
+                nc.tensor.matmul(
+                    neg_dz[:, c * P : (c + 1) * P],
+                    refs[t][:, h * BANK + c * P : h * BANK + (c + 1) * P],
+                    ident[:],
+                    start=(c == 0),
+                    stop=False,
+                    is_transpose=True,
+                )
+            for c in range(blocks):
+                nc.tensor.matmul(
+                    neg_dz[:, c * P : (c + 1) * P],
+                    neg_read[:, c * P : (c + 1) * P],
+                    ident[:],
+                    start=False,
+                    stop=(c == blocks - 1),
+                    is_transpose=True,
+                )
+            gate_t = work.tile([P, BANK], F32, name="gate_t", bufs=3)
+            nc.scalar.activation(gate_t[:], neg_dz[:], ACT.Sigmoid, scale=-1.0)
+            gate = psum.tile([P, BANK], F32, name="acc", bufs=5)
+            for c in range(blocks):
+                nc.tensor.transpose(gate[:, c * P : (c + 1) * P], gate_t[:, c * P : (c + 1) * P], ident[:])
+            nc.vector.scalar_tensor_tensor(hid_rows[h][:, t, :], neg_read[:], neg_unit[:, t : t + 1], gate[:], ALU.mult, ALU.mult)
+
+        def read_last_rows(t, h):
+            cols = slice(h * BANK, (h + 1) * BANK)
+            read = work.tile([P, BANK], F32, name="read")
+            dz = work.tile([P, BANK], F32, name="dz")
+            gate = work.tile([P, BANK], F32, name="gate")
+            nc.scalar.activation(read[:], pages[t][:].indirect(rd_sb[:, h * 32 : (h + 1) * 32]), ACT.Copy)
+            nc.vector.tensor_tensor(dz[:], read[:], refs[t][:, cols], ALU.subtract)
+            nc.scalar.activation(gate[:], dz[:], ACT.Sigmoid)
+            nc.vector.scalar_tensor_tensor(hid_rows[h][:, t, :], read[:], unit_sb[:, t : t + 1], gate[:], ALU.mult, ALU.mult)
+
+        def last_product(j):
+            h, c0 = divmod(j * OUT_COLS, BANK)
+            woven = work.tile([P, OUT_COLS, PACK], BF16, name="woven", align_bytes=64, bufs=4)
+            weave = nc.scalar.copy if j % 2 else nc.vector.tensor_copy
+            weave(
+                woven[:].rearrange("p (c i) t -> p c t i", i=4),
+                hid_rows[h][:, :, c0 : c0 + OUT_COLS].rearrange("p t (c i) -> p c t i", i=4),
+            )
+            codes = work.tile([P, OUT_COLS], U32, name="codes", align_bytes=64, bufs=4)
+            scales = work.tile([P, OUT_COLS], U8, name="scales", align_bytes=64, bufs=4)
+            nc.vector.quantize_mx(out=codes[:].bitcast(FP8X4), scales=scales[:], in_=woven[:].rearrange("p c t -> p (c t)"))
+            acc = psum.tile([P, N // P, OUT_COLS], F32, name="acc", bufs=5)
+            for m in range(N // P):
+                nc.tensor.matmul_mx(
+                    out=acc[:, m, :],
+                    lhsT=w3w[:, 2 * P * m : 2 * P * (m + 1)].bitcast(FP4X4),
+                    lhsT_scale=w3s[:, P * m : P * (m + 1)],
+                    rhs=codes[:].bitcast(FP8X4),
+                    rhs_scale=scales[:],
+                    start=True,
+                    stop=True,
+                )
+            res = work.tile([P, N // P, OUT_COLS], F32, name="res", bufs=4)
+            nc.scalar.copy(res[:], acc[:])
+            nc.sync.dma_start(
+                out=out.rearrange("(m p) r -> p m r", p=P)[:, :, j * OUT_COLS : (j + 1) * OUT_COLS], in_=res[:]
+            )
+
+        acts = [activations(0), activations(1)]
+        news = [blend(0, *acts[0])]
+        copies = [copied(news[0])]
+        acts.extend([activations(2), activations(3)])
+        for t in range(1, PACK):
+            news.append(blend(t, *acts[t]))
+            copies.append(copied(news[t]))
+            write_back(t - 1, news[t - 1], copies[t - 1])
+        write_back(PACK - 1, news[PACK - 1], copies[PACK - 1])
+        for t in range(PACK):
+            for h in range(U // BANK):
+                (read_rows if t + 1 < PACK else read_last_rows)(t, h)
+        for j in range(U // OUT_COLS):
+            last_product(j)

@@ -23,8 +23,8 @@ BANK = 512
 OUT_COLS = 256
 
 
-def load_scale_rows(queue, plane, scales):
-    for q in range(4):
+def load_scale_rows(queues, plane, scales):
+    for q, queue in enumerate(queues):
         queue.dma_start(out=plane[32 * q : 32 * q + 4, :].bitcast(I32), in_=scales[0, 4 * q : 4 * q + 4, :].bitcast(I32))
 
 
@@ -55,18 +55,19 @@ def tile_picked_yrwpage_gate_p_kernel(
         page_rows = page.rearrange("(p t) c -> t p c", t=PACK)
         ref_rows = ref.rearrange("(p t) c -> t p c", t=PACK)
 
-        for plane in (xs, w1s, w2s, w3s):
-            nc.vector.memset(plane[:].bitcast(I32), 0)
+        for plane in (xs, w1s, w2s):
+            nc.gpsimd.memset(plane[:].bitcast(I32), 0)
 
         nc.sync.dma_start(offs_sb[:], offs)
         nc.sync.dma_start(out=xw[:].bitcast(I32), in_=x_words[0].rearrange("p n t -> p (n t)").bitcast(I32))
-        load_scale_rows(nc.sync, xs, x_scales)
-        load_scale_rows(nc.gpsimd, w1s, w1_scales)
         nc.sync.dma_start(out=w1w[:].bitcast(I32), in_=w1_words[0].bitcast(I32))
         nc.sync.dma_start(out=w2w[:].bitcast(I32), in_=w2_words[0].bitcast(I32))
+        load_scale_rows([nc.sync] * 4, xs, x_scales)
+        load_scale_rows([nc.sync] * 4, w1s, w1_scales)
         nc.sync.dma_start(at_sb[:], at)
         nc.sync.dma_start(out=pages[0][:], in_=page_rows[0])
-        load_scale_rows(nc.sync, w2s, w2_scales)
+        load_scale_rows([nc.sync, nc.sync, nc.gpsimd, nc.gpsimd], w2s, w2_scales)
+        nc.gpsimd.memset(w3s[:].bitcast(I32), 0)
         nc.sync.dma_start(cop_sb[:], cop)
         for t in range(1, PACK):
             nc.sync.dma_start(out=pages[t][:], in_=page_rows[t])
@@ -75,7 +76,7 @@ def tile_picked_yrwpage_gate_p_kernel(
         for t in range(PACK):
             nc.sync.dma_start(out=refs[t][:], in_=ref_rows[t])
         nc.sync.dma_start(out=w3w[:].bitcast(I32), in_=w3_words[0].bitcast(I32))
-        load_scale_rows(nc.sync, w3s, w3_scales)
+        load_scale_rows([nc.sync] * 4, w3s, w3_scales)
 
         ident = keep.tile([P, P], F32, name="ident")
         make_identity(nc, ident[:])
@@ -122,7 +123,10 @@ def tile_picked_yrwpage_gate_p_kernel(
             th = work.tile([P, S], F32, name="th", bufs=4)
             old = None
             if t == 0:
-                old = keep.tile([P, S], F32, name="old")
+                old = keep.tile([P, S], F32, name="old0")
+                nc.vector.tensor_copy(old[:], pages[t][:].indirect(at_sb[:]))
+            if t == 1:
+                old = keep.tile([P, S], F32, name="old1")
                 nc.scalar.activation(old[:], pages[t][:].indirect(at_sb[:]), ACT.Copy)
             nc.scalar.activation(th[:], y[:], ACT.Tanh)
             nc.scalar.activation(fg[:], yg[:], ACT.Sigmoid)
@@ -136,7 +140,7 @@ def tile_picked_yrwpage_gate_p_kernel(
             kept = work.tile([P, S], F32, name="kept")
             neww = work.tile([P, S], F32, name="neww", bufs=4)
             for cols, entries in zip(halves, list_halves):
-                source = old[:, cols] if t == 0 else pages[t][:].indirect(at_sb[:, entries])
+                source = old[:, cols] if t < 2 else pages[t][:].indirect(at_sb[:, entries])
                 nc.vector.tensor_tensor(diff[:, cols], source, th[:, cols], ALU.subtract)
             for cols in halves:
                 nc.vector.tensor_tensor(kept[:, cols], diff[:, cols], fg[:, cols], ALU.mult)
@@ -149,6 +153,16 @@ def tile_picked_yrwpage_gate_p_kernel(
             for cols, entries in zip(halves, list_halves):
                 nc.scalar.activation(half[:, cols], neww[:].indirect(cop_sb[:, entries]), ACT.Copy, scale=0.5)
             return half
+
+        def write_back_on_scalar(t, neww):
+            twice = keep.tile([P, S], F32, name="twice")
+            wr2 = keep.tile([P, S], F32, name="wr2")
+            for cols in halves:
+                nc.vector.tensor_scalar(twice[:, cols], neww[:, cols], 2.0, None, ALU.mult)
+            for cols, entries in zip(halves, list_halves):
+                nc.vector.tensor_tensor(wr2[:, cols], neww[:].indirect(cop_sb[:, entries]), twice[:, cols], ALU.add)
+            for cols, entries in zip(halves, list_halves):
+                nc.scalar.activation(pages[t][:].indirect(at_sb[:, entries]), wr2[:, cols], ACT.Copy, scale=0.5)
 
         def write_back(t, neww, half):
             nc.vector.tensor_tensor(pages[t][:].indirect(at_sb[:]), neww[:], half[:], ALU.add)
@@ -190,7 +204,11 @@ def tile_picked_yrwpage_gate_p_kernel(
             read = work.tile([P, BANK], F32, name="read")
             dz = work.tile([P, BANK], F32, name="dz")
             gate = work.tile([P, BANK], F32, name="gate")
-            nc.scalar.activation(read[:], pages[t][:].indirect(rd_sb[:, h * 32 : (h + 1) * 32]), ACT.Copy)
+            picked = pages[t][:].indirect(rd_sb[:, h * 32 : (h + 1) * 32])
+            if h == 0:
+                nc.vector.tensor_copy(read[:], picked)
+            else:
+                nc.scalar.activation(read[:], picked, ACT.Copy)
             nc.vector.tensor_tensor(dz[:], read[:], refs[t][:, cols], ALU.subtract)
             nc.scalar.activation(gate[:], dz[:], ACT.Sigmoid)
             nc.vector.scalar_tensor_tensor(hid_rows[h][:, t, :], read[:], unit_sb[:, t : t + 1], gate[:], ALU.mult, ALU.mult)
@@ -218,20 +236,20 @@ def tile_picked_yrwpage_gate_p_kernel(
                     stop=True,
                 )
             res = work.tile([P, N // P, OUT_COLS], F32, name="res", bufs=4)
-            nc.scalar.copy(res[:], acc[:])
+            drain = nc.vector.tensor_copy if j == U // OUT_COLS - 1 else nc.scalar.copy
+            drain(res[:], acc[:])
             nc.sync.dma_start(
                 out=out.rearrange("(m p) r -> p m r", p=P)[:, :, j * OUT_COLS : (j + 1) * OUT_COLS], in_=res[:]
             )
 
-        acts = [activations(0), activations(1)]
-        news = [blend(0, *acts[0])]
-        copies = [copied(news[0])]
-        acts.extend([activations(2), activations(3)])
+        acts = [activations(t) for t in range(PACK)]
+        write_back_on_scalar(0, blend(0, *acts[0]))
+        pending = []
         for t in range(1, PACK):
-            news.append(blend(t, *acts[t]))
-            copies.append(copied(news[t]))
-            write_back(t - 1, news[t - 1], copies[t - 1])
-        write_back(PACK - 1, news[PACK - 1], copies[PACK - 1])
+            neww = blend(t, *acts[t])
+            pending.append((t, neww, copied(neww)))
+        for t, neww, half in pending:
+            write_back(t, neww, half)
         for t in range(PACK):
             for h in range(U // BANK):
                 (read_rows if t + 1 < PACK else read_last_rows)(t, h)

@@ -55,22 +55,21 @@ def tile_picked_yrwpage_gate_p_kernel(
         page_rows = page.rearrange("(p t) c -> t p c", t=PACK)
         ref_rows = ref.rearrange("(p t) c -> t p c", t=PACK)
 
-        for plane in (xs, w1s, w2s):
-            nc.gpsimd.memset(plane[:].bitcast(I32), 0)
+        for plane in (xs, w1s, w2s, w3s):
+            nc.vector.memset(plane[:].bitcast(I32), 0)
 
         nc.sync.dma_start(offs_sb[:], offs)
         nc.sync.dma_start(out=xw[:].bitcast(I32), in_=x_words[0].rearrange("p n t -> p (n t)").bitcast(I32))
-        nc.sync.dma_start(out=w1w[:].bitcast(I32), in_=w1_words[0].bitcast(I32))
-        nc.sync.dma_start(out=w2w[:].bitcast(I32), in_=w2_words[0].bitcast(I32))
         load_scale_rows([nc.sync] * 4, xs, x_scales)
-        load_scale_rows([nc.sync] * 4, w1s, w1_scales)
+        nc.sync.dma_start(out=w1w[:].bitcast(I32), in_=w1_words[0].bitcast(I32))
         nc.sync.dma_start(at_sb[:], at)
         nc.sync.dma_start(out=pages[0][:], in_=page_rows[0])
+        load_scale_rows([nc.sync] * 4, w1s, w1_scales)
+        nc.sync.dma_start(out=w2w[:].bitcast(I32), in_=w2_words[0].bitcast(I32))
         load_scale_rows([nc.sync, nc.sync, nc.gpsimd, nc.gpsimd], w2s, w2_scales)
-        nc.gpsimd.memset(w3s[:].bitcast(I32), 0)
-        nc.sync.dma_start(cop_sb[:], cop)
         for t in range(1, PACK):
             nc.sync.dma_start(out=pages[t][:], in_=page_rows[t])
+        nc.sync.dma_start(cop_sb[:], cop)
         nc.sync.dma_start(rd_sb[:], rd)
         nc.sync.dma_start(out=unit_sb[:], in_=unit.rearrange("(p t) o -> p (t o)", t=PACK))
         for t in range(PACK):
@@ -85,8 +84,8 @@ def tile_picked_yrwpage_gate_p_kernel(
 
         xq = keep.tile([P, S], U32, name="xq", align_bytes=64)
         xqs = keep.tile([P, S], U8, name="xqs", align_bytes=64)
-        nc.vector.tensor_copy(xqs[:], xs[:].indirect(offs_sb[:]))
         nc.vector.tensor_copy(xq[:], xw[:].indirect(offs_sb[:]))
+        nc.vector.tensor_copy(xqs[:], xs[:].indirect(offs_sb[:]))
 
         dealt = []
         for name, words, scales in (("w1", w1w, w1s), ("w2", w2w, w2s)):
@@ -104,7 +103,7 @@ def tile_picked_yrwpage_gate_p_kernel(
 
         def product(t, which):
             words_d, scales_d = dealt[which]
-            acc = psum.tile([P, S], F32, name="acc", bufs=5)
+            acc = psum.tile([P, S], F32, name="acc", bufs=4)
             nc.tensor.matmul_mx(
                 out=acc[:],
                 lhsT=words_d[:, 2 * P * t : 2 * P * (t + 1)].bitcast(FP4X4),
@@ -116,63 +115,53 @@ def tile_picked_yrwpage_gate_p_kernel(
             )
             return acc
 
-        def activations(t):
+        olds = [keep.tile([P, S], F32, name="old%d" % t) for t in range(2)]
+        nc.scalar.activation(olds[0][:], pages[0][:].indirect(at_sb[:]), ACT.Copy)
+        nc.vector.tensor_copy(olds[1][:], pages[1][:].indirect(at_sb[:]))
+
+        ths, fgs = [], []
+        for t in range(PACK):
             y = product(t, 0)
             yg = product(t, 1)
-            fg = work.tile([P, S], F32, name="fg", bufs=4)
-            th = work.tile([P, S], F32, name="th", bufs=4)
-            old = None
-            if t == 0:
-                old = keep.tile([P, S], F32, name="old0")
-                nc.vector.tensor_copy(old[:], pages[t][:].indirect(at_sb[:]))
-            if t == 1:
-                old = keep.tile([P, S], F32, name="old1")
-                nc.scalar.activation(old[:], pages[t][:].indirect(at_sb[:]), ACT.Copy)
-            nc.scalar.activation(th[:], y[:], ACT.Tanh)
-            nc.scalar.activation(fg[:], yg[:], ACT.Sigmoid)
-            return fg, th, old
+            ths.append(keep.tile([P, S], F32, name="th%d" % t))
+            fgs.append(keep.tile([P, S], F32, name="fg%d" % t))
+            nc.scalar.activation(ths[t][:], y[:], ACT.Tanh)
+            nc.scalar.activation(fgs[t][:], yg[:], ACT.Sigmoid)
 
-        halves = [slice(0, S // 2), slice(S // 2, S)]
-        list_halves = [slice(0, S // 32), slice(S // 32, S // 16)]
+        diffs = [keep.tile([P, S], F32, name="diff%d" % t) for t in range(PACK)]
+        blends = [keep.tile([P, 2 * S], F32, name="blend%d" % t) for t in range(PACK)]
+        halves = [keep.tile([P, S], F32, name="half%d" % t) for t in range(PACK)]
 
-        def blend(t, fg, th, old):
-            diff = work.tile([P, S], F32, name="diff")
-            kept = work.tile([P, S], F32, name="kept")
-            neww = work.tile([P, S], F32, name="neww", bufs=4)
-            for cols, entries in zip(halves, list_halves):
-                source = old[:, cols] if t < 2 else pages[t][:].indirect(at_sb[:, entries])
-                nc.vector.tensor_tensor(diff[:, cols], source, th[:, cols], ALU.subtract)
-            for cols in halves:
-                nc.vector.tensor_tensor(kept[:, cols], diff[:, cols], fg[:, cols], ALU.mult)
-            for cols in halves:
-                nc.vector.tensor_tensor(neww[:, cols], kept[:, cols], th[:, cols], ALU.add)
-            return neww
+        def subtract(t):
+            old = olds[t][:] if t < len(olds) else pages[t][:].indirect(at_sb[:])
+            nc.vector.tensor_tensor(diffs[t][:], old, ths[t][:], ALU.subtract)
 
-        def copied(neww):
-            half = work.tile([P, S], F32, name="half", bufs=4)
-            for cols, entries in zip(halves, list_halves):
-                nc.scalar.activation(half[:, cols], neww[:].indirect(cop_sb[:, entries]), ACT.Copy, scale=0.5)
-            return half
+        def forget(t):
+            nc.vector.tensor_tensor(blends[t][:, S:], diffs[t][:], fgs[t][:], ALU.mult)
 
-        def write_back_on_scalar(t, neww):
-            twice = keep.tile([P, S], F32, name="twice")
-            wr2 = keep.tile([P, S], F32, name="wr2")
-            for cols in halves:
-                nc.vector.tensor_scalar(twice[:, cols], neww[:, cols], 2.0, None, ALU.mult)
-            for cols, entries in zip(halves, list_halves):
-                nc.vector.tensor_tensor(wr2[:, cols], neww[:].indirect(cop_sb[:, entries]), twice[:, cols], ALU.add)
-            for cols, entries in zip(halves, list_halves):
-                nc.scalar.activation(pages[t][:].indirect(at_sb[:, entries]), wr2[:, cols], ACT.Copy, scale=0.5)
+        def renew(t):
+            nc.vector.tensor_tensor(blends[t][:, :S], blends[t][:, S:], ths[t][:], ALU.add)
 
-        def write_back(t, neww, half):
-            nc.vector.tensor_tensor(pages[t][:].indirect(at_sb[:]), neww[:], half[:], ALU.add)
+        def copied(t):
+            nc.scalar.activation(halves[t][:], blends[t][:].indirect(cop_sb[:]), ACT.Copy, scale=0.5)
+
+        def write_back_on_scalar(t):
+            wr = keep.tile([P, S], F32, name="wr")
+            nc.vector.tensor_tensor(wr[:], blends[t][:, :S], halves[t][:], ALU.add)
+            for h in range(2):
+                entries = slice(h * S // 32, (h + 1) * S // 32)
+                cols = slice(h * S // 2, (h + 1) * S // 2)
+                nc.scalar.activation(pages[t][:].indirect(at_sb[:, entries]), wr[:, cols], ACT.Copy)
+
+        def write_back(t):
+            nc.vector.tensor_tensor(pages[t][:].indirect(at_sb[:]), blends[t][:, :S], halves[t][:], ALU.add)
 
         hid_rows = [keep.tile([P, PACK, BANK], BF16, name="hid_rows%d" % h, align_bytes=64) for h in range(U // BANK)]
 
         def read_rows(t, h):
             neg_read = work.tile([P, BANK], F32, name="neg_read", bufs=8)
             nc.scalar.activation(neg_read[:], pages[t][:].indirect(rd_sb[:, h * 32 : (h + 1) * 32]), ACT.Copy, scale=-1.0)
-            neg_dz = psum.tile([P, BANK], F32, name="neg_dz", bufs=3)
+            neg_dz = psum.tile([P, BANK], F32, name="neg_dz", bufs=4)
             blocks = BANK // P
             for c in range(blocks):
                 nc.tensor.matmul(
@@ -194,7 +183,7 @@ def tile_picked_yrwpage_gate_p_kernel(
                 )
             gate_t = work.tile([P, BANK], F32, name="gate_t", bufs=3)
             nc.scalar.activation(gate_t[:], neg_dz[:], ACT.Sigmoid, scale=-1.0)
-            gate = psum.tile([P, BANK], F32, name="acc", bufs=5)
+            gate = psum.tile([P, BANK], F32, name="acc", bufs=4)
             for c in range(blocks):
                 nc.tensor.transpose(gate[:, c * P : (c + 1) * P], gate_t[:, c * P : (c + 1) * P], ident[:])
             nc.vector.scalar_tensor_tensor(hid_rows[h][:, t, :], neg_read[:], neg_unit[:, t : t + 1], gate[:], ALU.mult, ALU.mult)
@@ -205,10 +194,7 @@ def tile_picked_yrwpage_gate_p_kernel(
             dz = work.tile([P, BANK], F32, name="dz")
             gate = work.tile([P, BANK], F32, name="gate")
             picked = pages[t][:].indirect(rd_sb[:, h * 32 : (h + 1) * 32])
-            if h == 0:
-                nc.vector.tensor_copy(read[:], picked)
-            else:
-                nc.scalar.activation(read[:], picked, ACT.Copy)
+            nc.vector.tensor_copy(read[:], picked)
             nc.vector.tensor_tensor(dz[:], read[:], refs[t][:, cols], ALU.subtract)
             nc.scalar.activation(gate[:], dz[:], ACT.Sigmoid)
             nc.vector.scalar_tensor_tensor(hid_rows[h][:, t, :], read[:], unit_sb[:, t : t + 1], gate[:], ALU.mult, ALU.mult)
@@ -224,7 +210,7 @@ def tile_picked_yrwpage_gate_p_kernel(
             codes = work.tile([P, OUT_COLS], U32, name="codes", align_bytes=64, bufs=4)
             scales = work.tile([P, OUT_COLS], U8, name="scales", align_bytes=64, bufs=4)
             nc.vector.quantize_mx(out=codes[:].bitcast(FP8X4), scales=scales[:], in_=woven[:].rearrange("p c t -> p (c t)"))
-            acc = psum.tile([P, N // P, OUT_COLS], F32, name="acc", bufs=5)
+            acc = psum.tile([P, N // P, OUT_COLS], F32, name="acc", bufs=4)
             for m in range(N // P):
                 nc.tensor.matmul_mx(
                     out=acc[:, m, :],
@@ -242,14 +228,25 @@ def tile_picked_yrwpage_gate_p_kernel(
                 out=out.rearrange("(m p) r -> p m r", p=P)[:, :, j * OUT_COLS : (j + 1) * OUT_COLS], in_=res[:]
             )
 
-        acts = [activations(t) for t in range(PACK)]
-        write_back_on_scalar(0, blend(0, *acts[0]))
-        pending = []
+        subtract(0)
+        subtract(1)
+        forget(0)
+        forget(1)
+        renew(0)
+        subtract(2)
+        renew(1)
+        copied(0)
+        copied(1)
+        forget(2)
+        write_back_on_scalar(0)
+        renew(2)
+        subtract(3)
+        copied(2)
+        forget(3)
+        renew(3)
+        copied(3)
         for t in range(1, PACK):
-            neww = blend(t, *acts[t])
-            pending.append((t, neww, copied(neww)))
-        for t, neww, half in pending:
-            write_back(t, neww, half)
+            write_back(t)
         for t in range(PACK):
             for h in range(U // BANK):
                 (read_rows if t + 1 < PACK else read_last_rows)(t, h)

from contextlib import ExitStack

import concourse.mybir as mybir
from concourse.masks import make_identity

K, T, S, N, H, U = 512, 1024, 512, 256, 512, 1024
FLOPS = 2 * K * H * S * 2 + 2 * H * N * U

F32 = mybir.dt.float32
BF16 = mybir.dt.bfloat16
I32 = mybir.dt.int32
U32 = mybir.dt.uint32
U16 = mybir.dt.uint16
U8 = mybir.dt.uint8
FP8X4 = mybir.dt.float8_e4m3fn_x4
FP4X4 = mybir.dt.float4_e2m1fn_x4
ACT = mybir.ActivationFunctionType
ALU = mybir.AluOpType

P = 128
PACK = 4
BANK = 512
OUT_COLS = 256


def load_scale_rows(queues, plane, scales):
    for q, queue in enumerate(queues):
        queue.dma_start(out=plane[32 * q : 32 * q + 4, :].bitcast(I32), in_=scales[0, 4 * q : 4 * q + 4, :].bitcast(I32))


def tile_picked_yrwpage_gate_p_kernel(
    tc, x_words, x_scales, w1_words, w1_scales, w2_words, w2_scales, page, ref, unit, w3_words, w3_scales, offs, at, cop, rd, out
):
    nc = tc.nc
    with ExitStack() as ctx:
        keep = ctx.enter_context(tc.tile_pool(name="keep", bufs=1))
        work = ctx.enter_context(tc.tile_pool(name="work", bufs=2))
        psum = ctx.enter_context(tc.psum_pool(name="psum", bufs=2))

        offs_sb = keep.tile([P, S // 16], U16, name="offs_sb")
        at_sb = keep.tile([P, S // 16], U16, name="at_sb")
        cop_sb = keep.tile([P, S // 16], U16, name="cop_sb")
        rd_sb = keep.tile([P, U // 16], U16, name="rd_sb")
        xw = keep.tile([P, T], U32, name="xw", align_bytes=64)
        xs = keep.tile([P, T], U8, name="xs", align_bytes=64)
        w1w = keep.tile([P, 2 * H], U8, name="w1w", align_bytes=64)
        w2w = keep.tile([P, 2 * H], U8, name="w2w", align_bytes=64)
        w3w = keep.tile([P, 2 * N], U8, name="w3w", align_bytes=64)
        w1s = keep.tile([P, H], U8, name="w1s", align_bytes=64)
        w2s = keep.tile([P, H], U8, name="w2s", align_bytes=64)
        w3s = keep.tile([P, N], U8, name="w3s", align_bytes=64)
        unit_sb = keep.tile([P, PACK], F32, name="unit_sb")
        pages = [keep.tile([P, U], F32, name="page%d" % t) for t in range(PACK)]
        refs = [keep.tile([P, U], F32, name="ref%d" % t) for t in range(PACK)]
        page_rows = page.rearrange("(p t) c -> t p c", t=PACK)
        ref_rows = ref.rearrange("(p t) c -> t p c", t=PACK)

        for plane in (xs, w1s, w2s, w3s):
            nc.vector.memset(plane[:].bitcast(I32), 0)

        nc.sync.dma_start(offs_sb[:], offs)
        nc.sync.dma_start(out=xw[:].bitcast(I32), in_=x_words[0].rearrange("p n t -> p (n t)").bitcast(I32))
        load_scale_rows([nc.sync] * 4, xs, x_scales)
        nc.sync.dma_start(out=w1w[:].bitcast(I32), in_=w1_words[0].bitcast(I32))
        nc.sync.dma_start(at_sb[:], at)
        nc.sync.dma_start(out=pages[0][:], in_=page_rows[0])
        load_scale_rows([nc.sync] * 4, w1s, w1_scales)
        nc.sync.dma_start(out=w2w[:].bitcast(I32), in_=w2_words[0].bitcast(I32))
        load_scale_rows([nc.sync, nc.sync, nc.gpsimd, nc.gpsimd], w2s, w2_scales)
        for t in range(1, PACK):
            nc.sync.dma_start(out=pages[t][:], in_=page_rows[t])
        nc.sync.dma_start(cop_sb[:], cop)
        nc.sync.dma_start(rd_sb[:], rd)
        nc.sync.dma_start(out=unit_sb[:], in_=unit.rearrange("(p t) o -> p (t o)", t=PACK))
        for t in range(PACK):
            nc.sync.dma_start(out=refs[t][:], in_=ref_rows[t])
        nc.sync.dma_start(out=w3w[:].bitcast(I32), in_=w3_words[0].bitcast(I32))
        load_scale_rows([nc.sync] * 4, w3s, w3_scales)

        ident = keep.tile([P, P], F32, name="ident")
        make_identity(nc, ident[:])
        neg_unit = keep.tile([P, PACK], F32, name="neg_unit")
        nc.gpsimd.tensor_scalar(neg_unit[:], unit_sb[:], -1.0, 0.0, ALU.mult, ALU.add)

        xq = keep.tile([P, S], U32, name="xq", align_bytes=64)
        xqs = keep.tile([P, S], U8, name="xqs", align_bytes=64)
        nc.vector.tensor_copy(xq[:], xw[:].indirect(offs_sb[:]))
        nc.vector.tensor_copy(xqs[:], xs[:].indirect(offs_sb[:]))

        dealt = []
        for name, words, scales in (("w1", w1w, w1s), ("w2", w2w, w2s)):
            words_d = keep.tile([P, 2 * H], U8, name=name + "wd", align_bytes=64)
            scales_d = keep.tile([P, H], U8, name=name + "sd", align_bytes=64)
            nc.scalar.copy(
                words_d[:].bitcast(U16).rearrange("p (t m) -> p t m", t=PACK),
                words[:].bitcast(U16).rearrange("p (m t) -> p t m", t=PACK),
            )
            nc.vector.tensor_copy(
                scales_d[:].rearrange("p (t m) -> p t m", t=PACK),
                scales[:].rearrange("p (m t) -> p t m", t=PACK),
            )
            dealt.append((words_d, scales_d))

        def product(t, which):
            words_d, scales_d = dealt[which]
            acc = psum.tile([P, S], F32, name="acc", bufs=4)
            nc.tensor.matmul_mx(
                out=acc[:],
                lhsT=words_d[:, 2 * P * t : 2 * P * (t + 1)].bitcast(FP4X4),
                lhsT_scale=scales_d[:, P * t : P * (t + 1)],
                rhs=xq[:].bitcast(FP8X4),
                rhs_scale=xqs[:],
                start=True,
                stop=True,
            )
            return acc

        olds = [keep.tile([P, S], F32, name="old%d" % t) for t in range(2)]
        nc.scalar.activation(olds[0][:], pages[0][:].indirect(at_sb[:]), ACT.Copy)
        nc.vector.tensor_copy(olds[1][:], pages[1][:].indirect(at_sb[:]))

        ths, fgs = [], []
        for t in range(PACK):
            y = product(t, 0)
            yg = product(t, 1)
            ths.append(keep.tile([P, S], F32, name="th%d" % t))
            fgs.append(keep.tile([P, S], F32, name="fg%d" % t))
            nc.scalar.activation(ths[t][:], y[:], ACT.Tanh)
            nc.scalar.activation(fgs[t][:], yg[:], ACT.Sigmoid)

        diffs = [keep.tile([P, S], F32, name="diff%d" % t) for t in range(PACK)]
        blends = [keep.tile([P, 2 * S], F32, name="blend%d" % t) for t in range(PACK)]
        halves = [keep.tile([P, S], F32, name="half%d" % t) for t in range(PACK)]

        def subtract(t):
            old = olds[t][:] if t < len(olds) else pages[t][:].indirect(at_sb[:])
            nc.vector.tensor_tensor(diffs[t][:], old, ths[t][:], ALU.subtract)

        def forget(t):
            nc.vector.tensor_tensor(blends[t][:, S:], diffs[t][:], fgs[t][:], ALU.mult)

        def renew(t):
            nc.vector.tensor_tensor(blends[t][:, :S], blends[t][:, S:], ths[t][:], ALU.add)

        def copied(t):
            nc.scalar.activation(halves[t][:], blends[t][:].indirect(cop_sb[:]), ACT.Copy, scale=0.5)

        def write_back_on_scalar(t):
            wr = keep.tile([P, S], F32, name="wr")
            nc.vector.tensor_tensor(wr[:], blends[t][:, :S], halves[t][:], ALU.add)
            for h in range(2):
                entries = slice(h * S // 32, (h + 1) * S // 32)
                cols = slice(h * S // 2, (h + 1) * S // 2)
                nc.scalar.activation(pages[t][:].indirect(at_sb[:, entries]), wr[:, cols], ACT.Copy)

        def write_back(t):
            nc.vector.tensor_tensor(pages[t][:].indirect(at_sb[:]), blends[t][:, :S], halves[t][:], ALU.add)

        hid_rows = [keep.tile([P, PACK, BANK], BF16, name="hid_rows%d" % h, align_bytes=64) for h in range(U // BANK)]

        def read_rows(t, h):
            neg_read = work.tile([P, BANK], F32, name="neg_read", bufs=8)
            nc.scalar.activation(neg_read[:], pages[t][:].indirect(rd_sb[:, h * 32 : (h + 1) * 32]), ACT.Copy, scale=-1.0)
            neg_dz = psum.tile([P, BANK], F32, name="neg_dz", bufs=4)
            blocks = BANK // P
            for c in range(blocks):
                nc.tensor.matmul(
                    neg_dz[:, c * P : (c + 1) * P],
                    refs[t][:, h * BANK + c * P : h * BANK + (c + 1) * P],
                    ident[:],
                    start=(c == 0),
                    stop=False,
                    is_transpose=True,
                )
            for c in range(blocks):
                nc.tensor.matmul(
                    neg_dz[:, c * P : (c + 1) * P],
                    neg_read[:, c * P : (c + 1) * P],
                    ident[:],
                    start=False,
                    stop=(c == blocks - 1),
                    is_transpose=True,
                )
            gate_t = work.tile([P, BANK], F32, name="gate_t", bufs=3)
            nc.scalar.activation(gate_t[:], neg_dz[:], ACT.Sigmoid, scale=-1.0)
            gate = psum.tile([P, BANK], F32, name="acc", bufs=4)
            for c in range(blocks):
                nc.tensor.transpose(gate[:, c * P : (c + 1) * P], gate_t[:, c * P : (c + 1) * P], ident[:])
            nc.vector.scalar_tensor_tensor(hid_rows[h][:, t, :], neg_read[:], neg_unit[:, t : t + 1], gate[:], ALU.mult, ALU.mult)

        def read_last_rows(t, h):
            cols = slice(h * BANK, (h + 1) * BANK)
            read = work.tile([P, BANK], F32, name="read")
            dz = work.tile([P, BANK], F32, name="dz")
            gate = work.tile([P, BANK], F32, name="gate")
            picked = pages[t][:].indirect(rd_sb[:, h * 32 : (h + 1) * 32])
            nc.vector.tensor_copy(read[:], picked)
            nc.vector.tensor_tensor(dz[:], read[:], refs[t][:, cols], ALU.subtract)
            nc.scalar.activation(gate[:], dz[:], ACT.Sigmoid)
            nc.vector.scalar_tensor_tensor(hid_rows[h][:, t, :], read[:], unit_sb[:, t : t + 1], gate[:], ALU.mult, ALU.mult)

        def last_product(j):
            h, c0 = divmod(j * OUT_COLS, BANK)
            woven = work.tile([P, OUT_COLS, PACK], BF16, name="woven", align_bytes=64, bufs=4)
            weave = nc.scalar.copy if j % 2 else nc.vector.tensor_copy
            weave(
                woven[:].rearrange("p (c i) t -> p c t i", i=4),
                hid_rows[h][:, :, c0 : c0 + OUT_COLS].rearrange("p t (c i) -> p c t i", i=4),
            )
            codes = work.tile([P, OUT_COLS], U32, name="codes", align_bytes=64, bufs=4)
            scales = work.tile([P, OUT_COLS], U8, name="scales", align_bytes=64, bufs=4)
            nc.vector.quantize_mx(out=codes[:].bitcast(FP8X4), scales=scales[:], in_=woven[:].rearrange("p c t -> p (c t)"))
            acc = psum.tile([P, N // P, OUT_COLS], F32, name="acc", bufs=4)
            for m in range(N // P):
                nc.tensor.matmul_mx(
                    out=acc[:, m, :],
                    lhsT=w3w[:, 2 * P * m : 2 * P * (m + 1)].bitcast(FP4X4),
                    lhsT_scale=w3s[:, P * m : P * (m + 1)],
                    rhs=codes[:].bitcast(FP8X4),
                    rhs_scale=scales[:],
                    start=True,
                    stop=True,
                )
            res = work.tile([P, N // P, OUT_COLS], F32, name="res", bufs=4)
            drain = nc.vector.tensor_copy if j == U // OUT_COLS - 1 else nc.scalar.copy
            drain(res[:], acc[:])
            nc.sync.dma_start(
                out=out.rearrange("(m p) r -> p m r", p=P)[:, :, j * OUT_COLS : (j + 1) * OUT_COLS], in_=res[:]
            )

        subtract(0)
        subtract(1)
        forget(0)
        forget(1)
        renew(0)
        subtract(2)
        renew(1)
        copied(0)
        copied(1)
        forget(2)
        write_back_on_scalar(0)
        renew(2)
        subtract(3)
        copied(2)
        forget(3)
        renew(3)
        copied(3)
        for t in range(1, PACK):
            write_back(t)
        for t in range(PACK):
            for h in range(U // BANK):
                (read_rows if t + 1 < PACK else read_last_rows)(t, h)
        for j in range(U // OUT_COLS):
            last_product(j)
